import numpy as np
import ml_dtypes


def mxq(x, axis, fmt="e4m3"):
    dtype, down = {"e4m3": (ml_dtypes.float8_e4m3fn, 7), "e5m2": (ml_dtypes.float8_e5m2, 14)}[fmt]
    v = np.moveaxis(np.asarray(x, np.float32).astype(ml_dtypes.bfloat16).astype(np.float64), axis, -1)
    blocks = v.reshape(v.shape[:-1] + (-1, 32))
    amax = np.abs(blocks).max(-1, keepdims=True)
    byte = np.maximum(np.where(amax > 0, np.frexp(amax)[1] - 1 + 127, 0) - down, 1)
    scale = np.exp2(byte - 127.0)
    codes = (blocks / scale).astype(np.float32).astype(dtype).astype(np.float64)
    return np.moveaxis((codes * scale).reshape(v.shape), -1, axis)


WIDE = False


def mx_kscale(k):
    if not WIDE:
        return np.ones(k)
    levels = np.array([10, -10, 5, -5, 0])
    if k % 512:
        return np.exp2(np.random.permutation(np.resize(levels, k // 32))).repeat(32)
    a = np.empty((k // 512, 16))
    for p in range(k // 512):
        a[p, :8] = np.random.permutation(np.resize(levels, 8))
        for g in range(8):
            far = levels[np.abs(levels - a[p, g]) >= 10]
            a[p, g + 8] = far[np.random.randint(len(far))]
    return np.exp2(a.ravel()).repeat(32)


def f64(x):
    return np.asarray(x).astype(np.float64)


def striped(idx):
    return np.tile(idx.reshape(-1, 16).T, (8, 1)).astype(np.uint16)


def unstriped(offs):
    return offs[:16].T.reshape(-1).astype(np.int64)


def pack_weight(w):
    k, n = w.shape
    w = f64(np.asarray(w, np.float32).astype(ml_dtypes.bfloat16)).reshape(k // 32, 32, n)
    amax = np.abs(w).max(1)
    byte = np.clip(np.where(amax > 0, np.frexp(amax)[1] - 1 + 127 - 7, 1), 1, 254)
    scaled = (w * np.exp2(127.0 - byte)[:, None, :]).reshape(k, n).astype(np.float32)
    words = np.ascontiguousarray(scaled.reshape(k // 512, 128, 4, n).transpose(0, 1, 3, 2)).astype(ml_dtypes.float8_e4m3fn).view(np.uint8)
    return words, np.ascontiguousarray(byte.astype(np.uint8).reshape(k // 512, 16, n))


def unpack_weight(words, scales):
    g, p, n, _ = words.shape
    vals = np.ascontiguousarray(words).view(ml_dtypes.float8_e4m3fn).astype(np.float64) * np.repeat(np.exp2(scales.astype(np.float64) - 127.0), 8, axis=1)[..., None]
    return vals.transpose(0, 1, 3, 2).reshape(g * 512, n)


def relu(v):
    return np.maximum(v, 0.0)


K, T, S, N = 1024, 1024, 512, 256
P = 2 ** 7


def setup_inputs():
    n = np.random.standard_normal
    s = mx_kscale(K)[:, None]
    packed_xT = pack_weight(n((K, T)) * s)
    return {
        "x_words": packed_xT[0],
        "x_scales": packed_xT[1],
        "gate": np.tile(np.random.uniform(0.2, 1.0, S), (P, 1)).astype(np.float32),
        "res": n((N, T)).astype(np.float32),
        "w1": (n((K, N)) / np.sqrt(K) / s).astype(np.float32),
        "offs": striped(np.random.permutation(T)[:S]),
    }


def reference(x_words, x_scales, gate, res, w1, offs):
    r = f64(res)[:, unstriped(offs)]
    xq = unpack_weight(x_words, x_scales)[:, unstriped(offs)]
    y = relu(mxq(f64(w1), 0, "e4m3").T @ xq)
    out = f64(res).copy()
    out[:, unstriped(offs)] = r + y * f64(gate)[:1]
    return out

@@ -1,0 +1,119 @@
+from contextlib import ExitStack
+
+import concourse.mybir as mybir
+
+K, T, S, N = 1024, 1024, 512, 256
+FLOPS = 2 * K * S * N
+
+F32 = mybir.dt.float32
+BF16 = mybir.dt.bfloat16
+I32 = mybir.dt.int32
+U32 = mybir.dt.uint32
+U16 = mybir.dt.uint16
+U8 = mybir.dt.uint8
+FP8X4 = mybir.dt.float8_e4m3fn_x4
+ALU = mybir.AluOpType
+
+P = 128
+PACK = 4
+K_PASS = P * PACK
+PASSES = K // K_PASS
+BLOCKS = N // P
+QUADS = 4
+
+
+def tile_picked_modres_linrelu_p_kernel(tc, x_words, x_scales, gate, res, w1, offs, out):
+    nc = tc.nc
+    with ExitStack() as ctx:
+        keep = ctx.enter_context(tc.tile_pool(name="keep", bufs=1))
+        psum = ctx.enter_context(tc.psum_pool(name="psum", bufs=1))
+
+        offsets = keep.tile([P, S // 16], U16, name="offsets")
+        nc.sync.dma_start(offsets[:], offs)
+
+        scale_table = keep.tile([P, T], U8, name="scale_table", align_bytes=64)
+        nc.vector.memset(scale_table[:].bitcast(I32), 0)
+        for q in range(QUADS):
+            nc.sync.dma_start(
+                out=scale_table[32 * q : 32 * q + 4 * PASSES, :].bitcast(I32),
+                in_=x_scales[:, 4 * q : 4 * q + 4, :].bitcast(I32),
+            )
+
+        word_tables = []
+        for z in range(PASSES):
+            table = keep.tile([P, T], I32, name=f"word_table{z}", align_bytes=64)
+            nc.sync.dma_start(out=table[:], in_=x_words[z].rearrange("p t r -> p (t r)").bitcast(I32))
+            word_tables.append(table)
+
+        w_raw = []
+        for z in range(PASSES):
+            raw = keep.tile([P, PACK, N], F32, name=f"w_raw{z}")
+            rows = w1[z * K_PASS : (z + 1) * K_PASS, :]
+            nc.sync.dma_start(out=raw[:], in_=rows.rearrange("(p j) m -> p j m", j=PACK))
+            w_raw.append(raw)
+
+        stream = []
+        gates = keep.tile([P, S], F32, name="gates")
+        for b in range(BLOCKS):
+            rows = keep.tile([P, T], F32, name=f"stream{b}")
+            nc.sync.dma_start(out=rows[:], in_=res[b * P : (b + 1) * P, :])
+            stream.append(rows)
+            if b == 0:
+                nc.sync.dma_start(out=gates[:], in_=gate)
+
+        x_scale = keep.tile([P, S], U8, name="x_scale", align_bytes=64)
+        nc.vector.tensor_copy(x_scale[:], scale_table[:].indirect(offsets[:]))
+        x_codes = []
+        for z in range(PASSES):
+            picked = keep.tile([P, S], U32, name=f"x_codes{z}", align_bytes=64)
+            nc.vector.tensor_copy(picked[:], word_tables[z][:].bitcast(U32).indirect(offsets[:]))
+            x_codes.append(picked)
+
+        w_codes = []
+        w_scale = []
+        for z in range(PASSES):
+            grouped = keep.tile([P, N, PACK], BF16, name=f"w_grouped{z}", tag=f"reuse{z}", align_bytes=64)
+            for b in range(BLOCKS):
+                cols = slice(b * P, (b + 1) * P)
+                src = w_raw[z][:, :, cols].rearrange("p j (c i) -> p c j i", i=4)
+                dst = grouped[:, cols, :].rearrange("p (c i) j -> p c j i", i=4)
+                if z == PASSES - 1 and b == 0:
+                    nc.vector.tensor_copy(out=dst, in_=src)
+                else:
+                    nc.scalar.copy(out=dst, in_=src)
+            codes = keep.tile([P, N], U32, name=f"w_codes{z}", align_bytes=64)
+            scale = keep.tile([P, N], U8, name=f"w_scale{z}", align_bytes=64)
+            nc.vector.quantize_mx(
+                out=codes[:].bitcast(FP8X4), scales=scale[:], in_=grouped[:].rearrange("p m j -> p (m j)")
+            )
+            w_codes.append(codes)
+            w_scale.append(scale)
+
+        accs = [psum.tile([P, S], F32, name=f"acc{b}") for b in range(BLOCKS)]
+        for z in range(PASSES):
+            for b in range(BLOCKS):
+                cols = slice(b * P, (b + 1) * P)
+                nc.tensor.matmul_mx(
+                    out=accs[b][:],
+                    lhsT=w_codes[z][:, cols].bitcast(FP8X4),
+                    lhsT_scale=w_scale[z][:, cols],
+                    rhs=x_codes[z][:].bitcast(FP8X4),
+                    rhs_scale=x_scale[4 * z :, :],
+                    start=(z == 0),
+                    stop=(z == PASSES - 1),
+                )
+
+        olds = []
+        updates = []
+        for b in range(BLOCKS):
+            old = keep.tile([P, S], F32, name=f"old{b}", tag=f"reuse{PASSES - 1 - b}", align_bytes=64)
+            nc.vector.tensor_copy(old[:], stream[b][:].indirect(offsets[:]))
+            olds.append(old)
+            update = keep.tile([P, S], F32, name=f"update{b}")
+            nc.vector.scalar_tensor_tensor(
+                out=update[:], in0=accs[b][:], scalar=0.0, in1=gates[:], op0=ALU.max, op1=ALU.mult
+            )
+            updates.append(update)
+        for b in range(BLOCKS):
+            nc.vector.tensor_tensor(stream[b][:].indirect(offsets[:]), olds[b][:], updates[b][:], ALU.add)
+            nc.sync.dma_start(out=out[b * P : (b + 1) * P, :], in_=stream[b][:])

@@ -1,6 +1,7 @@
 from contextlib import ExitStack
 
 import concourse.mybir as mybir
+from concourse.masks import make_identity
 
 K, T, S, N = 1024, 1024, 512, 256
 FLOPS = 2 * K * S * N
@@ -13,12 +14,14 @@ U16 = mybir.dt.uint16
 U8 = mybir.dt.uint8
 FP8X4 = mybir.dt.float8_e4m3fn_x4
 ALU = mybir.AluOpType
+ACT = mybir.ActivationFunctionType
 
 P = 128
 PACK = 4
 K_PASS = P * PACK
 PASSES = K // K_PASS
 BLOCKS = N // P
+GROUPS = S // P
 QUADS = 4
 
 
@@ -33,41 +36,46 @@ def tile_picked_modres_linrelu_p_kernel(tc, x_words, x_scales, gate, res, w1, of
 
         scale_table = keep.tile([P, T], U8, name="scale_table", align_bytes=64)
         nc.vector.memset(scale_table[:].bitcast(I32), 0)
+        gate_rows = keep.tile([P, P], F32, name="gate_rows")
+        nc.gpsimd.memset(gate_rows[:], 0.0)
+        identity = keep.tile([P, P], F32, name="identity")
+        make_identity(nc, identity[:])
+
+        def load_words(z):
+            table = keep.tile([P, T], I32, name=f"word_table{z}", tag=f"table{z}", align_bytes=64)
+            nc.sync.dma_start(out=table[:], in_=x_words[z].rearrange("p t r -> p (t r)").bitcast(I32))
+            return table
+
+        word_tables = [load_words(0)]
         for q in range(QUADS):
             nc.sync.dma_start(
                 out=scale_table[32 * q : 32 * q + 4 * PASSES, :].bitcast(I32),
                 in_=x_scales[:, 4 * q : 4 * q + 4, :].bitcast(I32),
             )
-
-        word_tables = []
-        for z in range(PASSES):
-            table = keep.tile([P, T], I32, name=f"word_table{z}", align_bytes=64)
-            nc.sync.dma_start(out=table[:], in_=x_words[z].rearrange("p t r -> p (t r)").bitcast(I32))
-            word_tables.append(table)
-
+        nc.sync.dma_start(out=gate_rows[0:GROUPS, :], in_=gate[0].rearrange("(g t) -> g t", g=GROUPS))
         w_raw = []
         for z in range(PASSES):
             raw = keep.tile([P, PACK, N], F32, name=f"w_raw{z}")
             rows = w1[z * K_PASS : (z + 1) * K_PASS, :]
             nc.sync.dma_start(out=raw[:], in_=rows.rearrange("(p j) m -> p j m", j=PACK))
             w_raw.append(raw)
+        word_tables.append(load_words(1))
 
         stream = []
-        gates = keep.tile([P, S], F32, name="gates")
         for b in range(BLOCKS):
             rows = keep.tile([P, T], F32, name=f"stream{b}")
             nc.sync.dma_start(out=rows[:], in_=res[b * P : (b + 1) * P, :])
             stream.append(rows)
-            if b == 0:
-                nc.sync.dma_start(out=gates[:], in_=gate)
+
+        gate_turned = psum.tile([P, P], F32, name="gate_turned")
+        nc.tensor.transpose(gate_turned[:], gate_rows[:], identity[:])
+        gate_cols = keep.tile([P, GROUPS], F32, name="gate_cols")
+        nc.scalar.copy(out=gate_cols[:], in_=gate_turned[:, 0:GROUPS])
 
         x_scale = keep.tile([P, S], U8, name="x_scale", align_bytes=64)
+        x_codes = [keep.tile([P, S], U32, name="x_codes0", align_bytes=64)]
+        nc.vector.tensor_copy(x_codes[0][:], word_tables[0][:].bitcast(U32).indirect(offsets[:]))
         nc.vector.tensor_copy(x_scale[:], scale_table[:].indirect(offsets[:]))
-        x_codes = []
-        for z in range(PASSES):
-            picked = keep.tile([P, S], U32, name=f"x_codes{z}", align_bytes=64)
-            nc.vector.tensor_copy(picked[:], word_tables[z][:].bitcast(U32).indirect(offsets[:]))
-            x_codes.append(picked)
 
         w_codes = []
         w_scale = []
@@ -89,31 +97,51 @@ def tile_picked_modres_linrelu_p_kernel(tc, x_words, x_scales, gate, res, w1, of
             w_codes.append(codes)
             w_scale.append(scale)
 
-        accs = [psum.tile([P, S], F32, name=f"acc{b}") for b in range(BLOCKS)]
+        x_codes.append(keep.tile([P, S], U32, name="x_codes1", tag="reuse1", align_bytes=64))
+        for half in range(2):
+            entries = slice(half * S // 2, (half + 1) * S // 2)
+            lists = offsets[:, half * S // 32 : (half + 1) * S // 32]
+            nc.vector.tensor_copy(x_codes[1][:, entries], word_tables[1][:].bitcast(U32).indirect(lists))
+
+        accs = [psum.tile([P, N], F32, name=f"acc{g}") for g in range(GROUPS)]
         for z in range(PASSES):
-            for b in range(BLOCKS):
-                cols = slice(b * P, (b + 1) * P)
+            for g in range(GROUPS):
+                cols = slice(g * P, (g + 1) * P)
                 nc.tensor.matmul_mx(
-                    out=accs[b][:],
-                    lhsT=w_codes[z][:, cols].bitcast(FP8X4),
-                    lhsT_scale=w_scale[z][:, cols],
-                    rhs=x_codes[z][:].bitcast(FP8X4),
-                    rhs_scale=x_scale[4 * z :, :],
+                    out=accs[g][:],
+                    lhsT=x_codes[z][:, cols].bitcast(FP8X4),
+                    lhsT_scale=x_scale[4 * z :, cols],
+                    rhs=w_codes[z][:].bitcast(FP8X4),
+                    rhs_scale=w_scale[z][:],
                     start=(z == 0),
                     stop=(z == PASSES - 1),
                 )
 
-        olds = []
-        updates = []
+        olds = keep.tile([P, BLOCKS, S], F32, name="olds", tag="table1", align_bytes=64)
         for b in range(BLOCKS):
-            old = keep.tile([P, S], F32, name=f"old{b}", tag=f"reuse{PASSES - 1 - b}", align_bytes=64)
-            nc.vector.tensor_copy(old[:], stream[b][:].indirect(offsets[:]))
-            olds.append(old)
-            update = keep.tile([P, S], F32, name=f"update{b}")
-            nc.vector.scalar_tensor_tensor(
-                out=update[:], in0=accs[b][:], scalar=0.0, in1=gates[:], op0=ALU.max, op1=ALU.mult
-            )
-            updates.append(update)
+            nc.vector.tensor_copy(olds[:, b, :], stream[b][:].indirect(offsets[:]))
+
+        positive = keep.tile([P, GROUPS, N], F32, name="positive")
+        weighted = keep.tile([P, GROUPS, N], F32, name="weighted")
+        pieces = [range(0, 1), range(1, 2), range(2, 4)]
+        for piece in pieces:
+            width = len(piece) * P
+            turned = psum.tile([P, BLOCKS, width], F32, name=f"turned{piece.start}")
+            update = keep.tile([P, BLOCKS, width], F32, name=f"update{piece.start}")
+            for g in piece:
+                nc.scalar.activation(out=positive[:, g, :], in_=accs[g][:], func=ACT.Relu)
+            for g in piece:
+                nc.scalar.activation(
+                    out=weighted[:, g, :], in_=positive[:, g, :], func=ACT.Copy, scale=gate_cols[:, g : g + 1]
+                )
+            for b in range(BLOCKS):
+                for g in piece:
+                    at = (g - piece.start) * P
+                    nc.tensor.transpose(turned[:, b, at : at + P], weighted[:, g, b * P : (b + 1) * P], identity[:])
+            nc.scalar.copy(out=update[:], in_=turned[:])
+            entries = slice(piece.start * P, piece.stop * P)
+            lists = offsets[:, piece.start * P // 16 : piece.stop * P // 16]
+            for b in range(BLOCKS):
+                nc.vector.tensor_tensor(stream[b][:].indirect(lists), olds[:, b, entries], update[:, b, :], ALU.add)
         for b in range(BLOCKS):
-            nc.vector.tensor_tensor(stream[b][:].indirect(offsets[:]), olds[b][:], updates[b][:], ALU.add)
             nc.sync.dma_start(out=out[b * P : (b + 1) * P, :], in_=stream[b][:])

@@ -55,7 +55,7 @@ def tile_picked_modres_linrelu_p_kernel(tc, x_words, x_scales, gate, res, w1, of
         nc.sync.dma_start(out=gate_rows[0:GROUPS, :], in_=gate[0].rearrange("(g t) -> g t", g=GROUPS))
         w_raw = []
         for z in range(PASSES):
-            raw = keep.tile([P, PACK, N], F32, name=f"w_raw{z}")
+            raw = keep.tile([P, PACK, N], F32, name=f"w_raw{z}", tag=f"raw{z}", align_bytes=64)
             rows = w1[z * K_PASS : (z + 1) * K_PASS, :]
             nc.sync.dma_start(out=raw[:], in_=rows.rearrange("(p j) m -> p j m", j=PACK))
             w_raw.append(raw)
@@ -79,6 +79,7 @@ def tile_picked_modres_linrelu_p_kernel(tc, x_words, x_scales, gate, res, w1, of
 
         w_codes = []
         w_scale = []
+        groups = []
         for z in range(PASSES):
             grouped = keep.tile([P, N, PACK], BF16, name=f"w_grouped{z}", tag=f"reuse{z}", align_bytes=64)
             for b in range(BLOCKS):
@@ -89,6 +90,8 @@ def tile_picked_modres_linrelu_p_kernel(tc, x_words, x_scales, gate, res, w1, of
                     nc.vector.tensor_copy(out=dst, in_=src)
                 else:
                     nc.scalar.copy(out=dst, in_=src)
+            groups.append(grouped)
+        for z, grouped in enumerate(groups):
             codes = keep.tile([P, N], U32, name=f"w_codes{z}", align_bytes=64)
             scale = keep.tile([P, N], U8, name=f"w_scale{z}", align_bytes=64)
             nc.vector.quantize_mx(
@@ -97,7 +100,7 @@ def tile_picked_modres_linrelu_p_kernel(tc, x_words, x_scales, gate, res, w1, of
             w_codes.append(codes)
             w_scale.append(scale)
 
-        x_codes.append(keep.tile([P, S], U32, name="x_codes1", tag="reuse1", align_bytes=64))
+        x_codes.append(keep.tile([P, S], U32, name="x_codes1", tag="raw1", align_bytes=64))
         for half in range(2):
             entries = slice(half * S // 2, (half + 1) * S // 2)
             lists = offsets[:, half * S // 32 : (half + 1) * S // 32]
@@ -117,7 +120,7 @@ def tile_picked_modres_linrelu_p_kernel(tc, x_words, x_scales, gate, res, w1, of
                     stop=(z == PASSES - 1),
                 )
 
-        olds = keep.tile([P, BLOCKS, S], F32, name="olds", tag="table1", align_bytes=64)
+        olds = keep.tile([P, BLOCKS, S], F32, name="olds", tag="reuse1", align_bytes=64)
         for b in range(BLOCKS):
             nc.vector.tensor_copy(olds[:, b, :], stream[b][:].indirect(offsets[:]))
 

@@ -101,50 +101,60 @@ def tile_picked_modres_linrelu_p_kernel(tc, x_words, x_scales, gate, res, w1, of
             w_scale.append(scale)
 
         x_codes.append(keep.tile([P, S], U32, name="x_codes1", tag="raw1", align_bytes=64))
-        for half in range(2):
-            entries = slice(half * S // 2, (half + 1) * S // 2)
-            lists = offsets[:, half * S // 32 : (half + 1) * S // 32]
+        for first, last in ((0, 1), (1, 2), (2, 4)):
+            entries = slice(first * P, last * P)
+            lists = offsets[:, first * P // 16 : last * P // 16]
             nc.vector.tensor_copy(x_codes[1][:, entries], word_tables[1][:].bitcast(U32).indirect(lists))
 
-        accs = [psum.tile([P, N], F32, name=f"acc{g}") for g in range(GROUPS)]
+        def product(acc, g, z):
+            cols = slice(g * P, (g + 1) * P)
+            nc.tensor.matmul_mx(
+                out=acc[:],
+                lhsT=x_codes[z][:, cols].bitcast(FP8X4),
+                lhsT_scale=x_scale[4 * z :, cols],
+                rhs=w_codes[z][:].bitcast(FP8X4),
+                rhs_scale=w_scale[z][:],
+                start=(z == 0),
+                stop=(z == PASSES - 1),
+            )
+
+        accs = [psum.tile([P, N], F32, name=f"acc{g}", tag=f"acc{g}") for g in range(2)]
         for z in range(PASSES):
-            for g in range(GROUPS):
-                cols = slice(g * P, (g + 1) * P)
-                nc.tensor.matmul_mx(
-                    out=accs[g][:],
-                    lhsT=x_codes[z][:, cols].bitcast(FP8X4),
-                    lhsT_scale=x_scale[4 * z :, cols],
-                    rhs=w_codes[z][:].bitcast(FP8X4),
-                    rhs_scale=w_scale[z][:],
-                    start=(z == 0),
-                    stop=(z == PASSES - 1),
-                )
+            for g in range(2):
+                product(accs[g], g, z)
 
         olds = keep.tile([P, BLOCKS, S], F32, name="olds", tag="reuse1", align_bytes=64)
         for b in range(BLOCKS):
             nc.vector.tensor_copy(olds[:, b, :], stream[b][:].indirect(offsets[:]))
 
-        positive = keep.tile([P, GROUPS, N], F32, name="positive")
-        weighted = keep.tile([P, GROUPS, N], F32, name="weighted")
-        pieces = [range(0, 1), range(1, 2), range(2, 4)]
+        acc_tags = {2: "acc0", 3: "turned0"}
+        positive_tags = {2: "weighted0"}
+        pieces = [range(g, g + 1) for g in range(GROUPS)]
+        update = keep.tile([P, BLOCKS, S], F32, name="update")
+        cuts = [(0, 128, 256, 384, 512), (0, 128, 224, 320, 512)]
         for piece in pieces:
             width = len(piece) * P
-            turned = psum.tile([P, BLOCKS, width], F32, name=f"turned{piece.start}")
-            update = keep.tile([P, BLOCKS, width], F32, name=f"update{piece.start}")
+            weighted = []
             for g in piece:
-                nc.scalar.activation(out=positive[:, g, :], in_=accs[g][:], func=ACT.Relu)
-            for g in piece:
-                nc.scalar.activation(
-                    out=weighted[:, g, :], in_=positive[:, g, :], func=ACT.Copy, scale=gate_cols[:, g : g + 1]
+                if g >= 2:
+                    accs.append(psum.tile([P, N], F32, name=f"acc{g}", tag=acc_tags[g]))
+                    for z in range(PASSES):
+                        product(accs[g], g, z)
+                positive = keep.tile([P, N], F32, name=f"positive{g}", tag=positive_tags.get(g, f"positive{g}"))
+                nc.scalar.activation(out=positive[:], in_=accs[g][:], func=ACT.Relu)
+                scaled = keep.tile([P, N], F32, name=f"weighted{g}", tag=f"weighted{g}")
+                nc.scalar.activation(out=scaled[:], in_=positive[:], func=ACT.Copy, scale=gate_cols[:, g : g + 1])
+                weighted.append(scaled)
+            turned = psum.tile([P, BLOCKS, width], F32, name=f"turned{piece.start}", tag=f"turned{piece.start}")
+            for b in range(BLOCKS):
+                for i in range(len(piece)):
+                    nc.tensor.transpose(turned[:, b, i * P : (i + 1) * P], weighted[i][:, b * P : (b + 1) * P], identity[:])
+            nc.scalar.copy(out=update[:, :, piece.start * P : piece.stop * P], in_=turned[:])
+            for b in range(BLOCKS):
+                first, last = cuts[b][piece.start : piece.start + 2]
+                lists = offsets[:, first // 16 : last // 16]
+                nc.vector.tensor_tensor(
+                    stream[b][:].indirect(lists), olds[:, b, first:last], update[:, b, first:last], ALU.add
                 )
-            for b in range(BLOCKS):
-                for g in piece:
-                    at = (g - piece.start) * P
-                    nc.tensor.transpose(turned[:, b, at : at + P], weighted[:, g, b * P : (b + 1) * P], identity[:])
-            nc.scalar.copy(out=update[:], in_=turned[:])
-            entries = slice(piece.start * P, piece.stop * P)
-            lists = offsets[:, piece.start * P // 16 : piece.stop * P // 16]
-            for b in range(BLOCKS):
-                nc.vector.tensor_tensor(stream[b][:].indirect(lists), olds[:, b, entries], update[:, b, :], ALU.add)
         for b in range(BLOCKS):
             nc.sync.dma_start(out=out[b * P : (b + 1) * P, :], in_=stream[b][:])

@@ -31,9 +31,6 @@ def tile_picked_modres_linrelu_p_kernel(tc, x_words, x_scales, gate, res, w1, of
         keep = ctx.enter_context(tc.tile_pool(name="keep", bufs=1))
         psum = ctx.enter_context(tc.psum_pool(name="psum", bufs=1))
 
-        offsets = keep.tile([P, S // 16], U16, name="offsets")
-        nc.sync.dma_start(offsets[:], offs)
-
         scale_table = keep.tile([P, T], U8, name="scale_table", align_bytes=64)
         nc.vector.memset(scale_table[:].bitcast(I32), 0)
         gate_rows = keep.tile([P, P], F32, name="gate_rows")
@@ -46,19 +43,23 @@ def tile_picked_modres_linrelu_p_kernel(tc, x_words, x_scales, gate, res, w1, of
             nc.sync.dma_start(out=table[:], in_=x_words[z].rearrange("p t r -> p (t r)").bitcast(I32))
             return table
 
+        def load_w(z):
+            raw = keep.tile([P, PACK, N], F32, name=f"w_raw{z}", tag=f"raw{z}", align_bytes=64)
+            rows = w1[z * K_PASS : (z + 1) * K_PASS, :]
+            nc.sync.dma_start(out=raw[:], in_=rows.rearrange("(p j) m -> p j m", j=PACK))
+            return raw
+
         word_tables = [load_words(0)]
+        offsets = keep.tile([P, S // 16], U16, name="offsets")
+        nc.sync.dma_start(offsets[:], offs)
+        w_raw = [load_w(0)]
         for q in range(QUADS):
             nc.sync.dma_start(
                 out=scale_table[32 * q : 32 * q + 4 * PASSES, :].bitcast(I32),
                 in_=x_scales[:, 4 * q : 4 * q + 4, :].bitcast(I32),
             )
+        w_raw.append(load_w(1))
         nc.sync.dma_start(out=gate_rows[0:GROUPS, :], in_=gate[0].rearrange("(g t) -> g t", g=GROUPS))
-        w_raw = []
-        for z in range(PASSES):
-            raw = keep.tile([P, PACK, N], F32, name=f"w_raw{z}", tag=f"raw{z}", align_bytes=64)
-            rows = w1[z * K_PASS : (z + 1) * K_PASS, :]
-            nc.sync.dma_start(out=raw[:], in_=rows.rearrange("(p j) m -> p j m", j=PACK))
-            w_raw.append(raw)
         word_tables.append(load_words(1))
 
         stream = []
@@ -66,11 +67,6 @@ def tile_picked_modres_linrelu_p_kernel(tc, x_words, x_scales, gate, res, w1, of
             rows = keep.tile([P, T], F32, name=f"stream{b}")
             nc.sync.dma_start(out=rows[:], in_=res[b * P : (b + 1) * P, :])
             stream.append(rows)
-
-        gate_turned = psum.tile([P, P], F32, name="gate_turned")
-        nc.tensor.transpose(gate_turned[:], gate_rows[:], identity[:])
-        gate_cols = keep.tile([P, GROUPS], F32, name="gate_cols")
-        nc.scalar.copy(out=gate_cols[:], in_=gate_turned[:, 0:GROUPS])
 
         x_scale = keep.tile([P, S], U8, name="x_scale", align_bytes=64)
         x_codes = [keep.tile([P, S], U32, name="x_codes0", align_bytes=64)]
@@ -91,6 +87,12 @@ def tile_picked_modres_linrelu_p_kernel(tc, x_words, x_scales, gate, res, w1, of
                 else:
                     nc.scalar.copy(out=dst, in_=src)
             groups.append(grouped)
+
+        gate_turned = psum.tile([P, P], F32, name="gate_turned")
+        nc.tensor.transpose(gate_turned[:], gate_rows[:], identity[:])
+        gate_cols = keep.tile([P, GROUPS], F32, name="gate_cols")
+        nc.scalar.copy(out=gate_cols[:], in_=gate_turned[:, 0:GROUPS])
+
         for z, grouped in enumerate(groups):
             codes = keep.tile([P, N], U32, name=f"w_codes{z}", align_bytes=64)
             scale = keep.tile([P, N], U8, name=f"w_scale{z}", align_bytes=64)

@@ -52,13 +52,12 @@ def tile_picked_modres_linrelu_p_kernel(tc, x_words, x_scales, gate, res, w1, of
         word_tables = [load_words(0)]
         offsets = keep.tile([P, S // 16], U16, name="offsets")
         nc.sync.dma_start(offsets[:], offs)
-        w_raw = [load_w(0)]
         for q in range(QUADS):
             nc.sync.dma_start(
                 out=scale_table[32 * q : 32 * q + 4 * PASSES, :].bitcast(I32),
                 in_=x_scales[:, 4 * q : 4 * q + 4, :].bitcast(I32),
             )
-        w_raw.append(load_w(1))
+        w_raw = [load_w(z) for z in range(PASSES)]
         nc.sync.dma_start(out=gate_rows[0:GROUPS, :], in_=gate[0].rearrange("(g t) -> g t", g=GROUPS))
         word_tables.append(load_words(1))
 

@@ -29,6 +29,7 @@ def tile_picked_modres_linrelu_p_kernel(tc, x_words, x_scales, gate, res, w1, of
     nc = tc.nc
     with ExitStack() as ctx:
         keep = ctx.enter_context(tc.tile_pool(name="keep", bufs=1))
+        laid = ctx.enter_context(tc.tile_pool(name="laid", bufs=1))
         psum = ctx.enter_context(tc.psum_pool(name="psum", bufs=1))
 
         scale_table = keep.tile([P, T], U8, name="scale_table", align_bytes=64)
@@ -87,7 +88,7 @@ def tile_picked_modres_linrelu_p_kernel(tc, x_words, x_scales, gate, res, w1, of
                     nc.scalar.copy(out=dst, in_=src)
             groups.append(grouped)
 
-        gate_turned = psum.tile([P, P], F32, name="gate_turned")
+        gate_turned = psum.tile([P, P], F32, name="gate_turned", tag="bank7")
         nc.tensor.transpose(gate_turned[:], gate_rows[:], identity[:])
         gate_cols = keep.tile([P, GROUPS], F32, name="gate_cols")
         nc.scalar.copy(out=gate_cols[:], in_=gate_turned[:, 0:GROUPS])
@@ -107,55 +108,53 @@ def tile_picked_modres_linrelu_p_kernel(tc, x_words, x_scales, gate, res, w1, of
             lists = offsets[:, first * P // 16 : last * P // 16]
             nc.vector.tensor_copy(x_codes[1][:, entries], word_tables[1][:].bitcast(U32).indirect(lists))
 
-        def product(acc, g, z):
-            cols = slice(g * P, (g + 1) * P)
-            nc.tensor.matmul_mx(
-                out=acc[:],
-                lhsT=x_codes[z][:, cols].bitcast(FP8X4),
-                lhsT_scale=x_scale[4 * z :, cols],
-                rhs=w_codes[z][:].bitcast(FP8X4),
-                rhs_scale=w_scale[z][:],
-                start=(z == 0),
-                stop=(z == PASSES - 1),
-            )
-
-        accs = [psum.tile([P, N], F32, name=f"acc{g}", tag=f"acc{g}") for g in range(2)]
-        for z in range(PASSES):
-            for g in range(2):
-                product(accs[g], g, z)
-
         olds = keep.tile([P, BLOCKS, S], F32, name="olds", tag="reuse1", align_bytes=64)
         for b in range(BLOCKS):
             nc.vector.tensor_copy(olds[:, b, :], stream[b][:].indirect(offsets[:]))
 
-        acc_tags = {2: "acc0", 3: "turned0"}
-        positive_tags = {2: "weighted0"}
-        pieces = [range(g, g + 1) for g in range(GROUPS)]
         update = keep.tile([P, BLOCKS, S], F32, name="update")
-        cuts = [(0, 128, 256, 384, 512), (0, 128, 224, 320, 512)]
-        for piece in pieces:
-            width = len(piece) * P
-            weighted = []
-            for g in piece:
-                if g >= 2:
-                    accs.append(psum.tile([P, N], F32, name=f"acc{g}", tag=acc_tags[g]))
-                    for z in range(PASSES):
-                        product(accs[g], g, z)
-                positive = keep.tile([P, N], F32, name=f"positive{g}", tag=positive_tags.get(g, f"positive{g}"))
-                nc.scalar.activation(out=positive[:], in_=accs[g][:], func=ACT.Relu)
-                scaled = keep.tile([P, N], F32, name=f"weighted{g}", tag=f"weighted{g}")
-                nc.scalar.activation(out=scaled[:], in_=positive[:], func=ACT.Copy, scale=gate_cols[:, g : g + 1])
-                weighted.append(scaled)
-            turned = psum.tile([P, BLOCKS, width], F32, name=f"turned{piece.start}", tag=f"turned{piece.start}")
-            for b in range(BLOCKS):
-                for i in range(len(piece)):
-                    nc.tensor.transpose(turned[:, b, i * P : (i + 1) * P], weighted[i][:, b * P : (b + 1) * P], identity[:])
-            nc.scalar.copy(out=update[:, :, piece.start * P : piece.stop * P], in_=turned[:])
-            for b in range(BLOCKS):
-                first, last = cuts[b][piece.start : piece.start + 2]
-                lists = offsets[:, first // 16 : last // 16]
-                nc.vector.tensor_tensor(
-                    stream[b][:].indirect(lists), olds[:, b, first:last], update[:, b, first:last], ALU.add
+
+        def unit(g, blocks, acc_bank, turned_bank, positive_at, weighted_at):
+            entries = slice(g * P, (g + 1) * P)
+            rows = slice(blocks.start * P, blocks.stop * P)
+            width = rows.stop - rows.start
+            name = f"{g}{blocks.start}"
+            acc = psum.tile([P, width], F32, name=f"acc{name}", tag=f"bank{acc_bank}")
+            for z in range(PASSES):
+                nc.tensor.matmul_mx(
+                    out=acc[:],
+                    lhsT=x_codes[z][:, entries].bitcast(FP8X4),
+                    lhsT_scale=x_scale[4 * z :, entries],
+                    rhs=w_codes[z][:, rows].bitcast(FP8X4),
+                    rhs_scale=w_scale[z][:, rows],
+                    start=(z == 0),
+                    stop=(z == PASSES - 1),
                 )
+            positive = laid.tile([P, width], F32, name=f"positive{name}", offset=positive_at)
+            nc.scalar.activation(out=positive[:], in_=acc[:], func=ACT.Relu)
+            weighted = laid.tile([P, width], F32, name=f"weighted{name}", offset=weighted_at)
+            nc.scalar.activation(out=weighted[:], in_=positive[:], func=ACT.Copy, scale=gate_cols[:, g : g + 1])
+            turned = psum.tile([P, width // P, P], F32, name=f"turned{name}", tag=f"bank{turned_bank}")
+            for i in range(width // P):
+                nc.tensor.transpose(turned[:, i, :], weighted[:, i * P : (i + 1) * P], identity[:])
+            nc.scalar.copy(out=update[:, blocks, entries], in_=turned[:])
+
+        def scatter(b, first, last):
+            entries = slice(first * P, last * P)
+            lists = offsets[:, first * P // 16 : last * P // 16]
+            nc.vector.tensor_tensor(stream[b][:].indirect(lists), olds[:, b, entries], update[:, b, entries], ALU.add)
+
+        KB = 1024
+        unit(0, slice(0, 1), 0, 5, 0, KB)
+        scatter(0, 0, 1)
+        unit(0, slice(1, 2), 1, 6, 2 * KB, 4 * KB - 256)
+        scatter(1, 0, 1)
+        unit(1, slice(0, 2), 2, 7, 0, 5 * KB)
+        scatter(0, 1, 2)
+        scatter(1, 1, 2)
+        unit(2, slice(0, 2), 3, 0, 3 * KB, 6 * KB)
+        unit(3, slice(0, 2), 4, 1, 4 * KB, 7 * KB)
+        scatter(0, 2, 4)
+        scatter(1, 2, 4)
         for b in range(BLOCKS):
             nc.sync.dma_start(out=out[b * P : (b + 1) * P, :], in_=stream[b][:])

@@ -21,26 +21,23 @@ PACK = 4
 K_PASS = P * PACK
 PASSES = K // K_PASS
 BLOCKS = N // P
-GROUPS = S // P
 QUADS = 4
+HALF = S // 2
 
 
 def tile_picked_modres_linrelu_p_kernel(tc, x_words, x_scales, gate, res, w1, offs, out):
     nc = tc.nc
     with ExitStack() as ctx:
         keep = ctx.enter_context(tc.tile_pool(name="keep", bufs=1))
-        laid = ctx.enter_context(tc.tile_pool(name="laid", bufs=1))
         psum = ctx.enter_context(tc.psum_pool(name="psum", bufs=1))
 
         scale_table = keep.tile([P, T], U8, name="scale_table", align_bytes=64)
         nc.vector.memset(scale_table[:].bitcast(I32), 0)
-        gate_rows = keep.tile([P, P], F32, name="gate_rows")
-        nc.gpsimd.memset(gate_rows[:], 0.0)
         identity = keep.tile([P, P], F32, name="identity")
         make_identity(nc, identity[:])
 
         def load_words(z):
-            table = keep.tile([P, T], I32, name=f"word_table{z}", tag=f"table{z}", align_bytes=64)
+            table = keep.tile([P, T], I32, name=f"word_table{z}", align_bytes=64)
             nc.sync.dma_start(out=table[:], in_=x_words[z].rearrange("p t r -> p (t r)").bitcast(I32))
             return table
 
@@ -59,7 +56,8 @@ def tile_picked_modres_linrelu_p_kernel(tc, x_words, x_scales, gate, res, w1, of
                 in_=x_scales[:, 4 * q : 4 * q + 4, :].bitcast(I32),
             )
         w_raw = [load_w(z) for z in range(PASSES)]
-        nc.sync.dma_start(out=gate_rows[0:GROUPS, :], in_=gate[0].rearrange("(g t) -> g t", g=GROUPS))
+        gate_cols = keep.tile([P, S // P], F32, name="gate_cols")
+        nc.sync.dma_start(out=gate_cols[:], in_=gate[0].rearrange("(p c) -> p c", p=P))
         word_tables.append(load_words(1))
 
         stream = []
@@ -68,16 +66,17 @@ def tile_picked_modres_linrelu_p_kernel(tc, x_words, x_scales, gate, res, w1, of
             nc.sync.dma_start(out=rows[:], in_=res[b * P : (b + 1) * P, :])
             stream.append(rows)
 
+        def listed(first, last):
+            return offsets[:, first // 16 : last // 16]
+
         x_scale = keep.tile([P, S], U8, name="x_scale", align_bytes=64)
         x_codes = [keep.tile([P, S], U32, name="x_codes0", align_bytes=64)]
         nc.vector.tensor_copy(x_codes[0][:], word_tables[0][:].bitcast(U32).indirect(offsets[:]))
         nc.vector.tensor_copy(x_scale[:], scale_table[:].indirect(offsets[:]))
 
-        w_codes = []
-        w_scale = []
         groups = []
         for z in range(PASSES):
-            grouped = keep.tile([P, N, PACK], BF16, name=f"w_grouped{z}", tag=f"reuse{z}", align_bytes=64)
+            grouped = keep.tile([P, N, PACK], BF16, name=f"w_grouped{z}", tag=f"grouped{z}", align_bytes=64)
             for b in range(BLOCKS):
                 cols = slice(b * P, (b + 1) * P)
                 src = w_raw[z][:, :, cols].rearrange("p j (c i) -> p c j i", i=4)
@@ -88,11 +87,16 @@ def tile_picked_modres_linrelu_p_kernel(tc, x_words, x_scales, gate, res, w1, of
                     nc.scalar.copy(out=dst, in_=src)
             groups.append(grouped)
 
-        gate_turned = psum.tile([P, P], F32, name="gate_turned", tag="bank7")
-        nc.tensor.transpose(gate_turned[:], gate_rows[:], identity[:])
-        gate_cols = keep.tile([P, GROUPS], F32, name="gate_cols")
-        nc.scalar.copy(out=gate_cols[:], in_=gate_turned[:, 0:GROUPS])
+        gate_turned = psum.tile([P, S // P, P], F32, name="gate_turned")
+        for c in range(S // P):
+            nc.tensor.transpose(gate_turned[:, c, :], gate_cols[:, c : c + 1].to_broadcast([P, P]), identity[:])
+        gate_spread = keep.tile([P, S], F32, name="gate_spread")
+        nc.scalar.copy(
+            out=gate_spread[:].rearrange("q (p c) -> q p c", p=P), in_=gate_turned[:].rearrange("q c p -> q p c")
+        )
 
+        w_codes = []
+        w_scale = []
         for z, grouped in enumerate(groups):
             codes = keep.tile([P, N], U32, name=f"w_codes{z}", align_bytes=64)
             scale = keep.tile([P, N], U8, name=f"w_scale{z}", align_bytes=64)
@@ -103,58 +107,62 @@ def tile_picked_modres_linrelu_p_kernel(tc, x_words, x_scales, gate, res, w1, of
             w_scale.append(scale)
 
         x_codes.append(keep.tile([P, S], U32, name="x_codes1", tag="raw1", align_bytes=64))
-        for first, last in ((0, 1), (1, 2), (2, 4)):
-            entries = slice(first * P, last * P)
-            lists = offsets[:, first * P // 16 : last * P // 16]
-            nc.vector.tensor_copy(x_codes[1][:, entries], word_tables[1][:].bitcast(U32).indirect(lists))
+        halves = [slice(h * HALF, (h + 1) * HALF) for h in range(2)]
+        for entries in halves:
+            nc.vector.tensor_copy(
+                x_codes[1][:, entries], word_tables[1][:].bitcast(U32).indirect(listed(entries.start, entries.stop))
+            )
 
-        olds = keep.tile([P, BLOCKS, S], F32, name="olds", tag="reuse1", align_bytes=64)
+        def product(acc, b, z, entries, start, stop):
+            rows = slice(b * P, (b + 1) * P)
+            nc.tensor.matmul_mx(
+                out=acc,
+                lhsT=w_codes[z][:, rows].bitcast(FP8X4),
+                lhsT_scale=w_scale[z][:, rows],
+                rhs=x_codes[z][:, entries].bitcast(FP8X4),
+                rhs_scale=x_scale[4 * z :, entries],
+                start=start,
+                stop=stop,
+            )
+
+        accs = {}
         for b in range(BLOCKS):
-            nc.vector.tensor_copy(olds[:, b, :], stream[b][:].indirect(offsets[:]))
+            for h in range(2):
+                accs[b, h] = psum.tile([P, HALF], F32, name=f"acc{b}{h}")
+        for z in range(PASSES):
+            for h in range(2):
+                for b in range(BLOCKS):
+                    product(accs[b, h][:], b, z, halves[h], z == 0, z == PASSES - 1)
 
-        update = keep.tile([P, BLOCKS, S], F32, name="update")
+        update = [keep.tile([P, S], F32, name=f"update{b}") for b in range(BLOCKS)]
+        olds = [keep.tile([P, S], F32, name=f"olds{b}") for b in range(BLOCKS)]
+        sums = keep.tile([P, S], F32, name="sums")
 
-        def unit(g, blocks, acc_bank, turned_bank, positive_at, weighted_at):
-            entries = slice(g * P, (g + 1) * P)
-            rows = slice(blocks.start * P, blocks.stop * P)
-            width = rows.stop - rows.start
-            name = f"{g}{blocks.start}"
-            acc = psum.tile([P, width], F32, name=f"acc{name}", tag=f"bank{acc_bank}")
-            for z in range(PASSES):
-                nc.tensor.matmul_mx(
-                    out=acc[:],
-                    lhsT=x_codes[z][:, entries].bitcast(FP8X4),
-                    lhsT_scale=x_scale[4 * z :, entries],
-                    rhs=w_codes[z][:, rows].bitcast(FP8X4),
-                    rhs_scale=w_scale[z][:, rows],
-                    start=(z == 0),
-                    stop=(z == PASSES - 1),
-                )
-            positive = laid.tile([P, width], F32, name=f"positive{name}", offset=positive_at)
-            nc.scalar.activation(out=positive[:], in_=acc[:], func=ACT.Relu)
-            weighted = laid.tile([P, width], F32, name=f"weighted{name}", offset=weighted_at)
-            nc.scalar.activation(out=weighted[:], in_=positive[:], func=ACT.Copy, scale=gate_cols[:, g : g + 1])
-            turned = psum.tile([P, width // P, P], F32, name=f"turned{name}", tag=f"bank{turned_bank}")
-            for i in range(width // P):
-                nc.tensor.transpose(turned[:, i, :], weighted[:, i * P : (i + 1) * P], identity[:])
-            nc.scalar.copy(out=update[:, blocks, entries], in_=turned[:])
+        def gated(b, h):
+            nc.vector.scalar_tensor_tensor(
+                out=update[b][:, halves[h]],
+                in0=accs[b, h][:],
+                scalar=0.0,
+                in1=gate_spread[:, halves[h]],
+                op0=ALU.max,
+                op1=ALU.mult,
+            )
 
-        def scatter(b, first, last):
-            entries = slice(first * P, last * P)
-            lists = offsets[:, first * P // 16 : last * P // 16]
-            nc.vector.tensor_tensor(stream[b][:].indirect(lists), olds[:, b, entries], update[:, b, entries], ALU.add)
+        def add(first, last):
+            nc.vector.tensor_tensor(sums[:, first:last], olds[0][:, first:last], update[0][:, first:last], ALU.add)
 
-        KB = 1024
-        unit(0, slice(0, 1), 0, 5, 0, KB)
-        scatter(0, 0, 1)
-        unit(0, slice(1, 2), 1, 6, 2 * KB, 4 * KB - 256)
-        scatter(1, 0, 1)
-        unit(1, slice(0, 2), 2, 7, 0, 5 * KB)
-        scatter(0, 1, 2)
-        scatter(1, 1, 2)
-        unit(2, slice(0, 2), 3, 0, 3 * KB, 6 * KB)
-        unit(3, slice(0, 2), 4, 1, 4 * KB, 7 * KB)
-        scatter(0, 2, 4)
-        scatter(1, 2, 4)
+        for entries in halves:
+            nc.scalar.activation(olds[0][:, entries], stream[0][:].indirect(listed(entries.start, entries.stop)), ACT.Copy)
+        gated(0, 0)
+        gated(0, 1)
+        add(0, 128)
+        gated(1, 0)
+        add(128, 384)
+        gated(1, 1)
+        nc.vector.tensor_copy(olds[1][:], stream[1][:].indirect(offsets[:]))
+        add(384, 512)
+        for first, last in ((0, 128), (128, 384), (384, 512)):
+            nc.scalar.activation(stream[0][:].indirect(listed(first, last)), sums[:, first:last], ACT.Copy)
+        nc.vector.tensor_tensor(stream[1][:].indirect(offsets[:]), olds[1][:], update[1][:], ALU.add)
         for b in range(BLOCKS):
             nc.sync.dma_start(out=out[b * P : (b + 1) * P, :], in_=stream[b][:])

@@ -47,17 +47,17 @@ def tile_picked_modres_linrelu_p_kernel(tc, x_words, x_scales, gate, res, w1, of
             nc.sync.dma_start(out=raw[:], in_=rows.rearrange("(p j) m -> p j m", j=PACK))
             return raw
 
-        word_tables = [load_words(0)]
         offsets = keep.tile([P, S // 16], U16, name="offsets")
         nc.sync.dma_start(offsets[:], offs)
+        word_tables = [load_words(0)]
         for q in range(QUADS):
             nc.sync.dma_start(
                 out=scale_table[32 * q : 32 * q + 4 * PASSES, :].bitcast(I32),
                 in_=x_scales[:, 4 * q : 4 * q + 4, :].bitcast(I32),
             )
-        w_raw = [load_w(z) for z in range(PASSES)]
         gate_cols = keep.tile([P, S // P], F32, name="gate_cols")
         nc.sync.dma_start(out=gate_cols[:], in_=gate[0].rearrange("(p c) -> p c", p=P))
+        w_raw = [load_w(z) for z in range(PASSES)]
         word_tables.append(load_words(1))
 
         stream = []
@@ -87,14 +87,6 @@ def tile_picked_modres_linrelu_p_kernel(tc, x_words, x_scales, gate, res, w1, of
                     nc.scalar.copy(out=dst, in_=src)
             groups.append(grouped)
 
-        gate_turned = psum.tile([P, S // P, P], F32, name="gate_turned")
-        for c in range(S // P):
-            nc.tensor.transpose(gate_turned[:, c, :], gate_cols[:, c : c + 1].to_broadcast([P, P]), identity[:])
-        gate_spread = keep.tile([P, S], F32, name="gate_spread")
-        nc.scalar.copy(
-            out=gate_spread[:].rearrange("q (p c) -> q p c", p=P), in_=gate_turned[:].rearrange("q c p -> q p c")
-        )
-
         w_codes = []
         w_scale = []
         for z, grouped in enumerate(groups):
@@ -105,6 +97,14 @@ def tile_picked_modres_linrelu_p_kernel(tc, x_words, x_scales, gate, res, w1, of
             )
             w_codes.append(codes)
             w_scale.append(scale)
+
+        gate_turned = psum.tile([P, S // P, P], F32, name="gate_turned")
+        for c in range(S // P):
+            nc.tensor.transpose(gate_turned[:, c, :], gate_cols[:, c : c + 1].to_broadcast([P, P]), identity[:])
+        gate_spread = keep.tile([P, S], F32, name="gate_spread", tag="grouped0", align_bytes=64)
+        nc.scalar.copy(
+            out=gate_spread[:].rearrange("q (p c) -> q p c", p=P), in_=gate_turned[:].rearrange("q c p -> q p c")
+        )
 
         x_codes.append(keep.tile([P, S], U32, name="x_codes1", tag="raw1", align_bytes=64))
         halves = [slice(h * HALF, (h + 1) * HALF) for h in range(2)]
@@ -151,18 +151,22 @@ def tile_picked_modres_linrelu_p_kernel(tc, x_words, x_scales, gate, res, w1, of
         def add(first, last):
             nc.vector.tensor_tensor(sums[:, first:last], olds[0][:, first:last], update[0][:, first:last], ALU.add)
 
-        for entries in halves:
-            nc.scalar.activation(olds[0][:, entries], stream[0][:].indirect(listed(entries.start, entries.stop)), ACT.Copy)
+        def scalar_gather(b, first, last):
+            nc.scalar.activation(olds[b][:, first:last], stream[b][:].indirect(listed(first, last)), ACT.Copy)
+
+        shared = 128
+        scalar_gather(0, 0, HALF)
+        scalar_gather(0, HALF, S)
+        scalar_gather(1, 0, shared)
         gated(0, 0)
-        gated(0, 1)
-        add(0, 128)
         gated(1, 0)
-        add(128, 384)
+        add(0, HALF)
+        gated(0, 1)
         gated(1, 1)
-        nc.vector.tensor_copy(olds[1][:], stream[1][:].indirect(offsets[:]))
-        add(384, 512)
-        for first, last in ((0, 128), (128, 384), (384, 512)):
-            nc.scalar.activation(stream[0][:].indirect(listed(first, last)), sums[:, first:last], ACT.Copy)
+        nc.vector.tensor_copy(olds[1][:, shared:], stream[1][:].indirect(listed(shared, S)))
+        add(HALF, S)
+        for entries in halves:
+            nc.scalar.activation(stream[0][:].indirect(listed(entries.start, entries.stop)), sums[:, entries], ACT.Copy)
         nc.vector.tensor_tensor(stream[1][:].indirect(offsets[:]), olds[1][:], update[1][:], ALU.add)
         for b in range(BLOCKS):
             nc.sync.dma_start(out=out[b * P : (b + 1) * P, :], in_=stream[b][:])

@@ -23,6 +23,7 @@ PASSES = K // K_PASS
 BLOCKS = N // P
 QUADS = 4
 HALF = S // 2
+QUARTER = S // 4
 
 
 def tile_picked_modres_linrelu_p_kernel(tc, x_words, x_scales, gate, res, w1, offs, out):
@@ -154,19 +155,26 @@ def tile_picked_modres_linrelu_p_kernel(tc, x_words, x_scales, gate, res, w1, of
         def scalar_gather(b, first, last):
             nc.scalar.activation(olds[b][:, first:last], stream[b][:].indirect(listed(first, last)), ACT.Copy)
 
-        shared = 128
-        scalar_gather(0, 0, HALF)
-        scalar_gather(0, HALF, S)
-        scalar_gather(1, 0, shared)
+        def vector_gather(b, first, last):
+            nc.vector.tensor_copy(olds[b][:, first:last], stream[b][:].indirect(listed(first, last)))
+
+        def scalar_scatter(first, last):
+            nc.scalar.activation(stream[0][:].indirect(listed(first, last)), sums[:, first:last], ACT.Copy)
+
+        late = slice(HALF, HALF + QUARTER)
+        nc.vector.tensor_copy(olds[1][:, late], stream[0][:].indirect(listed(0, QUARTER)))
+        scalar_gather(0, QUARTER, S)
         gated(0, 0)
         gated(1, 0)
-        add(0, HALF)
+        nc.vector.tensor_tensor(sums[:, :QUARTER], olds[1][:, late], update[0][:, :QUARTER], ALU.add)
+        scalar_gather(1, 0, HALF)
+        scalar_scatter(0, QUARTER)
+        scalar_gather(1, HALF, HALF + QUARTER)
         gated(0, 1)
         gated(1, 1)
-        nc.vector.tensor_copy(olds[1][:, shared:], stream[1][:].indirect(listed(shared, S)))
-        add(HALF, S)
-        for entries in halves:
-            nc.scalar.activation(stream[0][:].indirect(listed(entries.start, entries.stop)), sums[:, entries], ACT.Copy)
+        add(QUARTER, S)
+        vector_gather(1, HALF + QUARTER, S)
+        scalar_scatter(QUARTER, S)
         nc.vector.tensor_tensor(stream[1][:].indirect(offsets[:]), olds[1][:], update[1][:], ALU.add)
         for b in range(BLOCKS):
             nc.sync.dma_start(out=out[b * P : (b + 1) * P, :], in_=stream[b][:])

@@ -24,6 +24,8 @@ BLOCKS = N // P
 QUADS = 4
 HALF = S // 2
 QUARTER = S // 4
+VECTOR_CAST = 160
+EARLY = 192
 
 
 def tile_picked_modres_linrelu_p_kernel(tc, x_words, x_scales, gate, res, w1, offs, out):
@@ -75,34 +77,33 @@ def tile_picked_modres_linrelu_p_kernel(tc, x_words, x_scales, gate, res, w1, of
         nc.vector.tensor_copy(x_codes[0][:], word_tables[0][:].bitcast(U32).indirect(offsets[:]))
         nc.vector.tensor_copy(x_scale[:], scale_table[:].indirect(offsets[:]))
 
-        groups = []
-        for z in range(PASSES):
-            grouped = keep.tile([P, N, PACK], BF16, name=f"w_grouped{z}", tag=f"grouped{z}", align_bytes=64)
-            for b in range(BLOCKS):
-                cols = slice(b * P, (b + 1) * P)
-                src = w_raw[z][:, :, cols].rearrange("p j (c i) -> p c j i", i=4)
-                dst = grouped[:, cols, :].rearrange("p (c i) j -> p c j i", i=4)
-                if z == PASSES - 1 and b == 0:
-                    nc.vector.tensor_copy(out=dst, in_=src)
-                else:
-                    nc.scalar.copy(out=dst, in_=src)
-            groups.append(grouped)
+        def cast(copy, z, cols, grouped):
+            src = w_raw[z][:, :, cols].rearrange("p j (c i) -> p c j i", i=4)
+            copy(out=grouped.rearrange("p (c i) j -> p c j i", i=4), in_=src)
 
-        w_codes = []
-        w_scale = []
-        for z, grouped in enumerate(groups):
-            codes = keep.tile([P, N], U32, name=f"w_codes{z}", align_bytes=64)
-            scale = keep.tile([P, N], U8, name=f"w_scale{z}", align_bytes=64)
+        def quantize(z, cols, grouped):
             nc.vector.quantize_mx(
-                out=codes[:].bitcast(FP8X4), scales=scale[:], in_=grouped[:].rearrange("p m j -> p (m j)")
+                out=w_codes[z][:, cols].bitcast(FP8X4),
+                scales=w_scale[z][:, cols],
+                in_=grouped.rearrange("p m j -> p (m j)"),
             )
-            w_codes.append(codes)
-            w_scale.append(scale)
+
+        w_codes = [keep.tile([P, N], U32, name=f"w_codes{z}", align_bytes=64) for z in range(PASSES)]
+        w_scale = [keep.tile([P, N], U8, name=f"w_scale{z}", align_bytes=64) for z in range(PASSES)]
+        for b in range(BLOCKS):
+            cols = slice(b * P, (b + 1) * P)
+            grouped = keep.tile([P, P, PACK], BF16, name=f"w_grouped0{b}", tag=f"grouped{b}", align_bytes=64)
+            cast(nc.scalar.copy, 0, cols, grouped[:])
+            quantize(0, cols, grouped[:])
+        grouped = keep.tile([P, N, PACK], BF16, name="w_grouped1", align_bytes=64)
+        cast(nc.vector.tensor_copy, 1, slice(0, VECTOR_CAST), grouped[:, :VECTOR_CAST, :])
+        cast(nc.scalar.copy, 1, slice(VECTOR_CAST, N), grouped[:, VECTOR_CAST:, :])
+        quantize(1, slice(0, N), grouped[:])
 
         gate_turned = psum.tile([P, S // P, P], F32, name="gate_turned")
         for c in range(S // P):
             nc.tensor.transpose(gate_turned[:, c, :], gate_cols[:, c : c + 1].to_broadcast([P, P]), identity[:])
-        gate_spread = keep.tile([P, S], F32, name="gate_spread", tag="grouped0", align_bytes=64)
+        gate_spread = keep.tile([P, S], F32, name="gate_spread", tag="grouped1", align_bytes=64)
         nc.scalar.copy(
             out=gate_spread[:].rearrange("q (p c) -> q p c", p=P), in_=gate_turned[:].rearrange("q c p -> q p c")
         )
@@ -130,10 +131,12 @@ def tile_picked_modres_linrelu_p_kernel(tc, x_words, x_scales, gate, res, w1, of
         for b in range(BLOCKS):
             for h in range(2):
                 accs[b, h] = psum.tile([P, HALF], F32, name=f"acc{b}{h}")
-        for z in range(PASSES):
+        for b in range(BLOCKS):
             for h in range(2):
-                for b in range(BLOCKS):
-                    product(accs[b, h][:], b, z, halves[h], z == 0, z == PASSES - 1)
+                product(accs[b, h][:], b, 0, halves[h], True, False)
+        for h in range(2):
+            for b in range(BLOCKS):
+                product(accs[b, h][:], b, 1, halves[h], False, True)
 
         update = [keep.tile([P, S], F32, name=f"update{b}") for b in range(BLOCKS)]
         olds = [keep.tile([P, S], F32, name=f"olds{b}") for b in range(BLOCKS)]
@@ -161,19 +164,19 @@ def tile_picked_modres_linrelu_p_kernel(tc, x_words, x_scales, gate, res, w1, of
         def scalar_scatter(first, last):
             nc.scalar.activation(stream[0][:].indirect(listed(first, last)), sums[:, first:last], ACT.Copy)
 
-        late = slice(HALF, HALF + QUARTER)
+        late = slice(EARLY, EARLY + QUARTER)
         nc.vector.tensor_copy(olds[1][:, late], stream[0][:].indirect(listed(0, QUARTER)))
         scalar_gather(0, QUARTER, S)
         gated(0, 0)
         gated(1, 0)
         nc.vector.tensor_tensor(sums[:, :QUARTER], olds[1][:, late], update[0][:, :QUARTER], ALU.add)
-        scalar_gather(1, 0, HALF)
+        scalar_gather(1, 0, EARLY)
         scalar_scatter(0, QUARTER)
-        scalar_gather(1, HALF, HALF + QUARTER)
+        scalar_gather(1, late.start, late.stop)
         gated(0, 1)
         gated(1, 1)
         add(QUARTER, S)
-        vector_gather(1, HALF + QUARTER, S)
+        vector_gather(1, late.stop, S)
         scalar_scatter(QUARTER, S)
         nc.vector.tensor_tensor(stream[1][:].indirect(offsets[:]), olds[1][:], update[1][:], ALU.add)
         for b in range(BLOCKS):

@@ -25,7 +25,8 @@ QUADS = 4
 HALF = S // 2
 QUARTER = S // 4
 VECTOR_CAST = 160
-EARLY = 192
+EARLY = 96
+SCALAR_SHARE = 256
 
 
 def tile_picked_modres_linrelu_p_kernel(tc, x_words, x_scales, gate, res, w1, offs, out):
@@ -50,9 +51,9 @@ def tile_picked_modres_linrelu_p_kernel(tc, x_words, x_scales, gate, res, w1, of
             nc.sync.dma_start(out=raw[:], in_=rows.rearrange("(p j) m -> p j m", j=PACK))
             return raw
 
+        word_tables = [load_words(0)]
         offsets = keep.tile([P, S // 16], U16, name="offsets")
         nc.sync.dma_start(offsets[:], offs)
-        word_tables = [load_words(0)]
         for q in range(QUADS):
             nc.sync.dma_start(
                 out=scale_table[32 * q : 32 * q + 4 * PASSES, :].bitcast(I32),
@@ -109,8 +110,8 @@ def tile_picked_modres_linrelu_p_kernel(tc, x_words, x_scales, gate, res, w1, of
         )
 
         x_codes.append(keep.tile([P, S], U32, name="x_codes1", tag="raw1", align_bytes=64))
-        halves = [slice(h * HALF, (h + 1) * HALF) for h in range(2)]
-        for entries in halves:
+        pieces = [slice(0, QUARTER), slice(QUARTER, HALF), slice(HALF, S)]
+        for entries in pieces:
             nc.vector.tensor_copy(
                 x_codes[1][:, entries], word_tables[1][:].bitcast(U32).indirect(listed(entries.start, entries.stop))
             )
@@ -127,27 +128,26 @@ def tile_picked_modres_linrelu_p_kernel(tc, x_words, x_scales, gate, res, w1, of
                 stop=stop,
             )
 
-        accs = {}
-        for b in range(BLOCKS):
-            for h in range(2):
-                accs[b, h] = psum.tile([P, HALF], F32, name=f"acc{b}{h}")
-        for b in range(BLOCKS):
-            for h in range(2):
-                product(accs[b, h][:], b, 0, halves[h], True, False)
-        for h in range(2):
-            for b in range(BLOCKS):
-                product(accs[b, h][:], b, 1, halves[h], False, True)
+        parts = [(0, pieces[0]), (0, pieces[1]), (1, slice(0, HALF)), (0, pieces[2]), (1, pieces[2])]
+        accs = [
+            psum.tile([P, entries.stop - entries.start], F32, name=f"acc{n}") for n, (b, entries) in enumerate(parts)
+        ]
+        for z in range(PASSES):
+            for acc, (b, entries) in zip(accs, parts):
+                product(acc[:], b, z, entries, z == 0, z == PASSES - 1)
 
         update = [keep.tile([P, S], F32, name=f"update{b}") for b in range(BLOCKS)]
         olds = [keep.tile([P, S], F32, name=f"olds{b}") for b in range(BLOCKS)]
+        first_update = olds[1][:, EARLY : EARLY + QUARTER]
         sums = keep.tile([P, S], F32, name="sums")
 
-        def gated(b, h):
+        def gated(n):
+            b, entries = parts[n]
             nc.vector.scalar_tensor_tensor(
-                out=update[b][:, halves[h]],
-                in0=accs[b, h][:],
+                out=first_update if n == 0 else update[b][:, entries],
+                in0=accs[n][:],
                 scalar=0.0,
-                in1=gate_spread[:, halves[h]],
+                in1=gate_spread[:, entries],
                 op0=ALU.max,
                 op1=ALU.mult,
             )
@@ -158,25 +158,23 @@ def tile_picked_modres_linrelu_p_kernel(tc, x_words, x_scales, gate, res, w1, of
         def scalar_gather(b, first, last):
             nc.scalar.activation(olds[b][:, first:last], stream[b][:].indirect(listed(first, last)), ACT.Copy)
 
-        def vector_gather(b, first, last):
-            nc.vector.tensor_copy(olds[b][:, first:last], stream[b][:].indirect(listed(first, last)))
-
         def scalar_scatter(first, last):
             nc.scalar.activation(stream[0][:].indirect(listed(first, last)), sums[:, first:last], ACT.Copy)
 
-        late = slice(EARLY, EARLY + QUARTER)
-        nc.vector.tensor_copy(olds[1][:, late], stream[0][:].indirect(listed(0, QUARTER)))
         scalar_gather(0, QUARTER, S)
-        gated(0, 0)
-        gated(1, 0)
-        nc.vector.tensor_tensor(sums[:, :QUARTER], olds[1][:, late], update[0][:, :QUARTER], ALU.add)
+        gated(0)
+        gated(1)
+        gated(2)
+        nc.vector.tensor_tensor(
+            sums[:, :QUARTER], stream[0][:].indirect(listed(0, QUARTER)), first_update, ALU.add
+        )
         scalar_gather(1, 0, EARLY)
         scalar_scatter(0, QUARTER)
-        scalar_gather(1, late.start, late.stop)
-        gated(0, 1)
-        gated(1, 1)
+        scalar_gather(1, EARLY, SCALAR_SHARE)
+        gated(3)
+        gated(4)
         add(QUARTER, S)
-        vector_gather(1, late.stop, S)
+        nc.vector.tensor_copy(olds[1][:, SCALAR_SHARE:], stream[1][:].indirect(listed(SCALAR_SHARE, S)))
         scalar_scatter(QUARTER, S)
         nc.vector.tensor_tensor(stream[1][:].indirect(offsets[:]), olds[1][:], update[1][:], ALU.add)
         for b in range(BLOCKS):

@@ -25,8 +25,8 @@ QUADS = 4
 HALF = S // 2
 QUARTER = S // 4
 VECTOR_CAST = 160
-EARLY = 96
-SCALAR_SHARE = 256
+EARLY = 128
+SCALAR_SHARE = 320
 
 
 def tile_picked_modres_linrelu_p_kernel(tc, x_words, x_scales, gate, res, w1, offs, out):

from contextlib import ExitStack

import concourse.mybir as mybir
from concourse.masks import make_identity

K, T, S, N = 1024, 1024, 512, 256
FLOPS = 2 * K * S * N

F32 = mybir.dt.float32
BF16 = mybir.dt.bfloat16
I32 = mybir.dt.int32
U32 = mybir.dt.uint32
U16 = mybir.dt.uint16
U8 = mybir.dt.uint8
FP8X4 = mybir.dt.float8_e4m3fn_x4
ALU = mybir.AluOpType
ACT = mybir.ActivationFunctionType

P = 128
PACK = 4
K_PASS = P * PACK
PASSES = K // K_PASS
BLOCKS = N // P
QUADS = 4
HALF = S // 2
QUARTER = S // 4
VECTOR_CAST = 160
EARLY = 128
SCALAR_SHARE = 320


def tile_picked_modres_linrelu_p_kernel(tc, x_words, x_scales, gate, res, w1, offs, out):
    nc = tc.nc
    with ExitStack() as ctx:
        keep = ctx.enter_context(tc.tile_pool(name="keep", bufs=1))
        psum = ctx.enter_context(tc.psum_pool(name="psum", bufs=1))

        scale_table = keep.tile([P, T], U8, name="scale_table", align_bytes=64)
        nc.vector.memset(scale_table[:].bitcast(I32), 0)
        identity = keep.tile([P, P], F32, name="identity")
        make_identity(nc, identity[:])

        def load_words(z):
            table = keep.tile([P, T], I32, name=f"word_table{z}", align_bytes=64)
            nc.sync.dma_start(out=table[:], in_=x_words[z].rearrange("p t r -> p (t r)").bitcast(I32))
            return table

        def load_w(z):
            raw = keep.tile([P, PACK, N], F32, name=f"w_raw{z}", tag=f"raw{z}", align_bytes=64)
            rows = w1[z * K_PASS : (z + 1) * K_PASS, :]
            nc.sync.dma_start(out=raw[:], in_=rows.rearrange("(p j) m -> p j m", j=PACK))
            return raw

        word_tables = [load_words(0)]
        offsets = keep.tile([P, S // 16], U16, name="offsets")
        nc.sync.dma_start(offsets[:], offs)
        for q in range(QUADS):
            nc.sync.dma_start(
                out=scale_table[32 * q : 32 * q + 4 * PASSES, :].bitcast(I32),
                in_=x_scales[:, 4 * q : 4 * q + 4, :].bitcast(I32),
            )
        gate_cols = keep.tile([P, S // P], F32, name="gate_cols")
        nc.sync.dma_start(out=gate_cols[:], in_=gate[0].rearrange("(p c) -> p c", p=P))
        w_raw = [load_w(z) for z in range(PASSES)]
        word_tables.append(load_words(1))

        stream = []
        for b in range(BLOCKS):
            rows = keep.tile([P, T], F32, name=f"stream{b}")
            nc.sync.dma_start(out=rows[:], in_=res[b * P : (b + 1) * P, :])
            stream.append(rows)

        def listed(first, last):
            return offsets[:, first // 16 : last // 16]

        x_scale = keep.tile([P, S], U8, name="x_scale", align_bytes=64)
        x_codes = [keep.tile([P, S], U32, name="x_codes0", align_bytes=64)]
        nc.vector.tensor_copy(x_codes[0][:], word_tables[0][:].bitcast(U32).indirect(offsets[:]))
        nc.vector.tensor_copy(x_scale[:], scale_table[:].indirect(offsets[:]))

        def cast(copy, z, cols, grouped):
            src = w_raw[z][:, :, cols].rearrange("p j (c i) -> p c j i", i=4)
            copy(out=grouped.rearrange("p (c i) j -> p c j i", i=4), in_=src)

        def quantize(z, cols, grouped):
            nc.vector.quantize_mx(
                out=w_codes[z][:, cols].bitcast(FP8X4),
                scales=w_scale[z][:, cols],
                in_=grouped.rearrange("p m j -> p (m j)"),
            )

        w_codes = [keep.tile([P, N], U32, name=f"w_codes{z}", align_bytes=64) for z in range(PASSES)]
        w_scale = [keep.tile([P, N], U8, name=f"w_scale{z}", align_bytes=64) for z in range(PASSES)]
        for b in range(BLOCKS):
            cols = slice(b * P, (b + 1) * P)
            grouped = keep.tile([P, P, PACK], BF16, name=f"w_grouped0{b}", tag=f"grouped{b}", align_bytes=64)
            cast(nc.scalar.copy, 0, cols, grouped[:])
            quantize(0, cols, grouped[:])
        grouped = keep.tile([P, N, PACK], BF16, name="w_grouped1", align_bytes=64)
        cast(nc.vector.tensor_copy, 1, slice(0, VECTOR_CAST), grouped[:, :VECTOR_CAST, :])
        cast(nc.scalar.copy, 1, slice(VECTOR_CAST, N), grouped[:, VECTOR_CAST:, :])
        quantize(1, slice(0, N), grouped[:])

        gate_turned = psum.tile([P, S // P, P], F32, name="gate_turned")
        for c in range(S // P):
            nc.tensor.transpose(gate_turned[:, c, :], gate_cols[:, c : c + 1].to_broadcast([P, P]), identity[:])
        gate_spread = keep.tile([P, S], F32, name="gate_spread", tag="grouped1", align_bytes=64)
        nc.scalar.copy(
            out=gate_spread[:].rearrange("q (p c) -> q p c", p=P), in_=gate_turned[:].rearrange("q c p -> q p c")
        )

        x_codes.append(keep.tile([P, S], U32, name="x_codes1", tag="raw1", align_bytes=64))
        pieces = [slice(0, QUARTER), slice(QUARTER, HALF), slice(HALF, S)]
        for entries in pieces:
            nc.vector.tensor_copy(
                x_codes[1][:, entries], word_tables[1][:].bitcast(U32).indirect(listed(entries.start, entries.stop))
            )

        def product(acc, b, z, entries, start, stop):
            rows = slice(b * P, (b + 1) * P)
            nc.tensor.matmul_mx(
                out=acc,
                lhsT=w_codes[z][:, rows].bitcast(FP8X4),
                lhsT_scale=w_scale[z][:, rows],
                rhs=x_codes[z][:, entries].bitcast(FP8X4),
                rhs_scale=x_scale[4 * z :, entries],
                start=start,
                stop=stop,
            )

        parts = [(0, pieces[0]), (0, pieces[1]), (1, slice(0, HALF)), (0, pieces[2]), (1, pieces[2])]
        accs = [
            psum.tile([P, entries.stop - entries.start], F32, name=f"acc{n}") for n, (b, entries) in enumerate(parts)
        ]
        for z in range(PASSES):
            for acc, (b, entries) in zip(accs, parts):
                product(acc[:], b, z, entries, z == 0, z == PASSES - 1)

        update = [keep.tile([P, S], F32, name=f"update{b}") for b in range(BLOCKS)]
        olds = [keep.tile([P, S], F32, name=f"olds{b}") for b in range(BLOCKS)]
        first_update = olds[1][:, EARLY : EARLY + QUARTER]
        sums = keep.tile([P, S], F32, name="sums")

        def gated(n):
            b, entries = parts[n]
            nc.vector.scalar_tensor_tensor(
                out=first_update if n == 0 else update[b][:, entries],
                in0=accs[n][:],
                scalar=0.0,
                in1=gate_spread[:, entries],
                op0=ALU.max,
                op1=ALU.mult,
            )

        def add(first, last):
            nc.vector.tensor_tensor(sums[:, first:last], olds[0][:, first:last], update[0][:, first:last], ALU.add)

        def scalar_gather(b, first, last):
            nc.scalar.activation(olds[b][:, first:last], stream[b][:].indirect(listed(first, last)), ACT.Copy)

        def scalar_scatter(first, last):
            nc.scalar.activation(stream[0][:].indirect(listed(first, last)), sums[:, first:last], ACT.Copy)

        scalar_gather(0, QUARTER, S)
        gated(0)
        gated(1)
        gated(2)
        nc.vector.tensor_tensor(
            sums[:, :QUARTER], stream[0][:].indirect(listed(0, QUARTER)), first_update, ALU.add
        )
        scalar_gather(1, 0, EARLY)
        scalar_scatter(0, QUARTER)
        scalar_gather(1, EARLY, SCALAR_SHARE)
        gated(3)
        gated(4)
        add(QUARTER, S)
        nc.vector.tensor_copy(olds[1][:, SCALAR_SHARE:], stream[1][:].indirect(listed(SCALAR_SHARE, S)))
        scalar_scatter(QUARTER, S)
        nc.vector.tensor_tensor(stream[1][:].indirect(offsets[:]), olds[1][:], update[1][:], ALU.add)
        for b in range(BLOCKS):
            nc.sync.dma_start(out=out[b * P : (b + 1) * P, :], in_=stream[b][:])
